import numpy as np
import ml_dtypes


def mxq(x, axis, fmt="e4m3"):
    dtype, down = {"e4m3": (ml_dtypes.float8_e4m3fn, 7), "e5m2": (ml_dtypes.float8_e5m2, 14)}[fmt]
    v = np.moveaxis(np.asarray(x, np.float32).astype(ml_dtypes.bfloat16).astype(np.float64), axis, -1)
    blocks = v.reshape(v.shape[:-1] + (-1, 32))
    amax = np.abs(blocks).max(-1, keepdims=True)
    byte = np.maximum(np.where(amax > 0, np.frexp(amax)[1] - 1 + 127, 0) - down, 1)
    scale = np.exp2(byte - 127.0)
    codes = (blocks / scale).astype(np.float32).astype(dtype).astype(np.float64)
    return np.moveaxis((codes * scale).reshape(v.shape), -1, axis)


WIDE = False


def mx_kscale(k):
    if not WIDE:
        return np.ones(k)
    levels = np.array([10, -10, 5, -5, 0])
    if k % 512:
        return np.exp2(np.random.permutation(np.resize(levels, k // 32))).repeat(32)
    a = np.empty((k // 512, 16))
    for p in range(k // 512):
        a[p, :8] = np.random.permutation(np.resize(levels, 8))
        for g in range(8):
            far = levels[np.abs(levels - a[p, g]) >= 10]
            a[p, g + 8] = far[np.random.randint(len(far))]
    return np.exp2(a.ravel()).repeat(32)


def f64(x):
    return np.asarray(x).astype(np.float64)


E2M1 = np.array([0.0, 0.5, 1.0, 1.5, 2.0, 3.0, 4.0, 6.0, -0.0, -0.5, -1.0, -1.5, -2.0, -3.0, -4.0, -6.0])


def pack_weight(w, fmt):
    k, n = w.shape
    w = f64(np.asarray(w, np.float32).astype(ml_dtypes.bfloat16)).reshape(k // 32, 32, n)
    amax = np.abs(w).max(1)
    if fmt == "e4m3":
        byte = np.frexp(amax)[1] - 1 + 127 - 7
    else:
        mant, ex = np.frexp(amax / 6.0)
        byte = np.where(mant > 0.5, ex, ex - 1) + 127
    byte = np.clip(np.where(amax > 0, byte, 1), 1, 254)
    scaled = (w * np.exp2(127.0 - byte)[:, None, :]).reshape(k, n).astype(np.float32)
    by_word = np.ascontiguousarray(scaled.reshape(k // 512, 128, 4, n).transpose(0, 1, 3, 2))
    if fmt == "e4m3":
        words = by_word.astype(ml_dtypes.float8_e4m3fn).view(np.uint8)
    else:
        c = by_word.astype(ml_dtypes.float4_e2m1fn).view(np.uint8) & 0xF
        words = (c[..., 0::2] | (c[..., 1::2] << 4)).reshape(k // 512, 128, 2 * n)
    return np.ascontiguousarray(words), np.ascontiguousarray(byte.astype(np.uint8).reshape(k // 512, 16, n))


def unpack_weight(words, scales, fmt):
    g, _, n = scales.shape
    words = np.ascontiguousarray(words).reshape(g, 128, n, -1)
    if fmt == "e4m3":
        vals = words.view(ml_dtypes.float8_e4m3fn).astype(np.float64)
    else:
        nib = np.empty((g, 128, n, 4), np.uint8)
        nib[..., 0::2] = words & 0xF
        nib[..., 1::2] = words >> 4
        vals = E2M1[nib]
    vals = vals * np.repeat(np.exp2(scales.astype(np.float64) - 127.0), 8, axis=1)[..., None]
    return vals.transpose(0, 1, 3, 2).reshape(g * 512, n)


def planes(y):
    n, m = y.shape
    v = y.astype(np.float32).astype(ml_dtypes.bfloat16).astype(np.float64).reshape(n // 32, 32, m)
    top = np.abs(v).max(1)
    byte = np.clip(np.where(top > 0, np.frexp(top)[1] - 1 + 127 - 7, 1), 1, 254)
    codes = (v * np.exp2(127.0 - byte)[:, None, :]).reshape(n, m).astype(np.float32).astype(ml_dtypes.float8_e4m3fn).view(np.uint8)
    words = codes.reshape(n // 512, 128, 4, m).transpose(0, 1, 3, 2)
    return np.ascontiguousarray(words), np.ascontiguousarray(byte.astype(np.uint8).reshape(n // 512, 16, m))


def silu(v):
    return v / (1.0 + np.exp(-np.maximum(v, -700.0)))


D, K, M, T = 256, 512, 1024, 1536


def setup_inputs():
    n = np.random.standard_normal
    s = mx_kscale(K)[:, None]
    p_w0 = pack_weight(n((K, M)) / np.sqrt(K) / s, "e2m1")
    p_w1 = pack_weight(n((K, M)) / np.sqrt(K) / s, "e4m3")
    return {
        "x": (n((K, T + 2 * D)) * s).astype(np.float32),
        "w0_words": p_w0[0],
        "w0_scales": p_w0[1],
        "w1_words": p_w1[0],
        "w1_scales": p_w1[1],
        "w2": (n((K, M)) / np.sqrt(K) / s).astype(np.float32),
        "b": (0.3 * n(1024)).astype(np.float32),
    }


def reference(x, w0_words, w0_scales, w1_words, w1_scales, w2, b):
    x_ = mxq(f64(x), 0, "e4m3")
    w0_ = unpack_weight(w0_words, w0_scales, "e2m1")
    w1_ = unpack_weight(w1_words, w1_scales, "e4m3")
    w2_ = mxq(f64(w2), 0, "e4m3")
    y = w0_.T @ x_[:, :T] + w1_.T @ x_[:, D:D + T] + w2_.T @ x_[:, 2 * D:]
    out_0 = silu(y + f64(b)[:, None])
    return (out_0,) + planes(out_0)

@@ -1,0 +1,262 @@
+from contextlib import ExitStack
+
+import concourse.mybir as mybir
+
+D, K, M, T = 256, 512, 1024, 1536
+FLOPS = 2 * 3 * K * M * T
+
+F32 = mybir.dt.float32
+BF16 = mybir.dt.bfloat16
+I32 = mybir.dt.int32
+U8 = mybir.dt.uint8
+FP8X4 = mybir.dt.float8_e4m3fn_x4
+FP4X4 = mybir.dt.float4_e2m1fn_x4
+SILU = mybir.ActivationFunctionType.Silu
+
+P = 128
+PACK = 4
+NT = 512
+HALF = 256
+GROUPS = M // (P * PACK)
+
+
+def tile_mix_dconv_fm_pl_silu_kernel(
+    tc, x, w0_words, w0_scales, w1_words, w1_scales, w2, b, out_0, out_1, out_2
+):
+    nc = tc.nc
+    x_rows = x.rearrange("(p j) t -> p j t", j=PACK)
+    w2_rows = w2.rearrange("(p j) n -> p j n", j=PACK)
+    out_rows = out_0.rearrange("(a p r) t -> a p r t", a=GROUPS, r=PACK)
+    out_words = out_1.rearrange("a p t i -> p a (t i)").bitcast(I32)
+    out_scales = out_2.rearrange("a q t -> q a t").bitcast(I32)
+
+    with ExitStack() as ctx:
+        sb = ctx.enter_context(tc.tile_pool(name="sb", bufs=1))
+        psum = ctx.enter_context(tc.psum_pool(name="psum", bufs=1))
+        ctx.enter_context(tc.manual_schedule())
+
+        def tile(name, shape, dtype):
+            return sb.tile(shape, dtype, name=name, align_bytes=64)
+
+        warm_in = tile("warm_in", [P, 1], F32)
+        warm_out = tile("warm_out", [P, 1], F32)
+        bias = tile("bias", [P, GROUPS, 2 * PACK], F32)
+        scale_raw = tile("scale_raw", [P, 2, M], U8)
+        w0_raw = tile("w0_raw", [P, 2 * M], U8)
+        w1_raw = tile("w1_raw", [P, M], I32)
+        w2_raw = [tile("w2_raw%d" % a, [P, PACK, NT], F32) for a in range(GROUPS)]
+        x_raw = [tile("x_raw%d" % c, [P, PACK, NT], F32) for c in range(4)]
+        w0_codes = tile("w0_codes", [P, 2 * M], U8)
+        w1_codes = tile("w1_codes", [P, M], I32)
+        w2_codes = tile("w2_codes", [P, M], I32)
+        w_scale = [tile("w_scale%d" % tap, [P, M], U8) for tap in range(3)]
+        x_codes = tile("x_codes", [P, T + 2 * D], I32)
+        x_scale = tile("x_scale", [P, T + 2 * D], U8)
+        y = {(a, tt): tile("y%d%d" % (a, tt), [P, PACK, NT], F32) for a in range(GROUPS) for tt in range(3)}
+        y_codes = [tile("y_codes0", [P, GROUPS, 2 * NT], I32), tile("y_codes1", [P, GROUPS, NT], I32)]
+        y_scale = [tile("y_scale0", [P, GROUPS, 2 * NT], U8), tile("y_scale1", [P, GROUPS, NT], U8)]
+        staged = {}
+        banks = {}
+
+        def load_scales(tap, scales, quad):
+            nc.sync.dma_start(
+                out=scale_raw[32 * quad : 32 * quad + 4, tap, :].bitcast(I32),
+                in_=scales[0, 4 * quad : 4 * quad + 4, :].bitcast(I32),
+            )
+
+        def load_x(c):
+            nc.sync.dma_start(out=x_raw[c][:], in_=x_rows[:, :, NT * c : NT * (c + 1)])
+
+        def load_w2(a):
+            nc.sync.dma_start(out=w2_raw[a][:], in_=w2_rows[:, :, NT * a : NT * (a + 1)])
+
+        def copy(engine, out, in_):
+            if engine == "scalar":
+                nc.scalar.copy(out=out, in_=in_)
+            else:
+                nc.vector.tensor_copy(out=out, in_=in_)
+
+        def interleave(engine, key, src, h):
+            grouped = tile("g_%s" % key, [P, HALF, PACK], BF16)
+            copy(
+                engine,
+                grouped[:].rearrange("p (c i) j -> p c j i", i=4),
+                src[:, :, HALF * h : HALF * (h + 1)].rearrange("p j (c i) -> p c j i", i=4),
+            )
+            staged[key] = grouped[:].rearrange("p c j -> p (c j)")
+
+        def quantize(key, codes, scales):
+            nc.vector.quantize_mx(out=codes.bitcast(FP8X4), scales=scales, in_=staged[key])
+
+        def cast_x(engine, c, h):
+            interleave(engine, "x%d%d" % (c, h), x_raw[c], h)
+
+        def quant_x(c, h):
+            cols = slice(NT * c + HALF * h, NT * c + HALF * (h + 1))
+            quantize("x%d%d" % (c, h), x_codes[:, cols], x_scale[:, cols])
+
+        def cast_w2(engine, a, h):
+            grouped = tile("g_w%d%d" % (a, h), [P, 2, P, PACK], BF16)
+            copy(
+                engine,
+                grouped[:].rearrange("p r m j -> p m r j"),
+                w2_raw[a][:].rearrange("p j (m r) -> p m r j", r=PACK)[:, :, 2 * h : 2 * h + 2, :],
+            )
+            staged["w%d%d" % (a, h)] = grouped[:].rearrange("p r m j -> p (r m j)")
+
+        def quant_w2(a, h):
+            cols = slice(NT * a + HALF * h, NT * a + HALF * (h + 1))
+            quantize("w%d%d" % (a, h), w2_codes[:, cols], w_scale[2][:, cols])
+
+        def deal_scales(tap):
+            nc.vector.tensor_copy(
+                out=w_scale[tap][:].rearrange("p (a r m) -> p a r m", a=GROUPS, r=PACK),
+                in_=scale_raw[:, tap, :].rearrange("p (a m r) -> p a r m", a=GROUPS, r=PACK),
+            )
+
+        def deal_w0(a):
+            cols = slice(2 * NT * a, 2 * NT * (a + 1))
+            nc.vector.tensor_copy(
+                out=w0_codes[:, cols].rearrange("p (r m e) -> p r m e", r=PACK, e=2),
+                in_=w0_raw[:, cols].rearrange("p (m r e) -> p r m e", r=PACK, e=2),
+            )
+
+        def deal_w1():
+            nc.vector.tensor_copy(
+                out=w1_codes[:].rearrange("p (a r m) -> p a m r", a=GROUPS, r=PACK),
+                in_=w1_raw[:].rearrange("p (a m r) -> p a m r", a=GROUPS, r=PACK),
+            )
+
+        def open_banks(a, tt, first):
+            for r in range(PACK):
+                banks[a, tt, r] = psum.tile([P, NT], F32, name="acc%d%d%d" % (a, tt, r), tag="bank%d" % (first + r))
+
+        def tap_pass(tap, a, tt, r):
+            n0 = NT * a + P * r
+            if tap == 0:
+                lhsT = w0_codes[:, 2 * n0 : 2 * (n0 + P)].bitcast(FP4X4)
+            else:
+                lhsT = (w1_codes if tap == 1 else w2_codes)[:, n0 : n0 + P].bitcast(FP8X4)
+            cols = slice(NT * tt + D * tap, NT * (tt + 1) + D * tap)
+            nc.tensor.matmul_mx(
+                out=banks[a, tt, r][:],
+                lhsT=lhsT,
+                lhsT_scale=w_scale[tap][:, n0 : n0 + P],
+                rhs=x_codes[:, cols].bitcast(FP8X4),
+                rhs_scale=x_scale[:, cols],
+                start=(tap == 0),
+                stop=(tap == 2),
+            )
+
+        def tap_sweep(tap, a, tt):
+            for r in range(PACK):
+                tap_pass(tap, a, tt, r)
+
+        def silu_out(a, tt, r):
+            nc.scalar.activation(out=y[a, tt][:, r, :], in_=banks[a, tt, r][:], func=SILU, bias=bias[:, a, r : r + 1])
+
+        def finish(a, tt):
+            for r in range(PACK):
+                tap_pass(2, a, tt, r)
+                silu_out(a, tt, r)
+
+        def whole(a, tt, first):
+            open_banks(a, tt, first)
+            for r in range(PACK):
+                for tap in range(3):
+                    tap_pass(tap, a, tt, r)
+                silu_out(a, tt, r)
+
+        def requantize(a, tt):
+            for h in range(2):
+                interleave("vector", "y%d%d%d" % (a, tt, h), y[a, tt], h)
+            for h in range(2):
+                c0 = NT * (tt % 2) + HALF * h
+                quantize("y%d%d%d" % (a, tt, h), y_codes[tt // 2][:, a, c0 : c0 + HALF], y_scale[tt // 2][:, a, c0 : c0 + HALF])
+
+        def both_halves(cast, quant, c):
+            cast("vector", c, 0)
+            cast("vector", c, 1)
+            quant(c, 0)
+            quant(c, 1)
+
+        def store_y(a, tt):
+            nc.sync.dma_start(out=out_rows[a, :, :, NT * tt : NT * (tt + 1)], in_=y[a, tt][:])
+
+        def store_scales(part):
+            c0, c1 = (0, 2 * NT // 4) if part == 0 else (2 * NT // 4, T // 4)
+            for quad in range(4):
+                nc.sync.dma_start(
+                    out=out_scales[4 * quad : 4 * quad + 4, :, c0:c1],
+                    in_=y_scale[part][32 * quad : 32 * quad + 4, :, :].bitcast(I32),
+                )
+
+        nc.vector.memset(scale_raw[:].rearrange("p s n -> p (s n)").bitcast(I32), 0)
+        nc.vector.memset(warm_in[:], 0.0)
+        nc.scalar.activation(out=warm_out[:], in_=warm_in[:], func=SILU)
+        nc.sync.dma_start(out=w0_raw[:].bitcast(I32), in_=w0_words[0].bitcast(I32))
+        for quad in range(4):
+            load_scales(0, w0_scales, quad)
+        load_x(0)
+        nc.sync.dma_start(out=w1_raw[:], in_=w1_words[0].rearrange("p n i -> p (n i)").bitcast(I32))
+        for quad in range(4):
+            load_scales(1, w1_scales, quad)
+        load_x(1)
+        nc.sync.dma_start(out=bias[:, :, 0:PACK], in_=b.rearrange("(a p r) -> p a r", a=GROUPS, r=PACK))
+        load_w2(0)
+        load_x(2)
+        load_w2(1)
+        load_x(3)
+
+        deal_scales(0)
+        deal_w0(0)
+        cast_x("vector", 0, 0)
+        cast_x("scalar", 0, 1)
+        deal_w0(1)
+        quant_x(0, 0)
+        quant_x(0, 1)
+        open_banks(0, 0, 0)
+        open_banks(1, 0, 4)
+        tap_sweep(0, 0, 0)
+        tap_sweep(0, 1, 0)
+        deal_w1()
+        deal_scales(1)
+        cast_x("vector", 1, 0)
+        cast_x("scalar", 1, 1)
+        quant_x(1, 0)
+        tap_sweep(1, 0, 0)
+        tap_sweep(1, 1, 0)
+        quant_x(1, 1)
+        cast_w2("vector", 0, 0)
+        cast_w2("scalar", 0, 1)
+        quant_w2(0, 0)
+        quant_w2(0, 1)
+        finish(0, 0)
+        store_y(0, 0)
+        open_banks(0, 1, 0)
+        tap_sweep(0, 0, 1)
+        both_halves(cast_x, quant_x, 2)
+        tap_sweep(1, 0, 1)
+        finish(0, 1)
+        store_y(0, 1)
+        both_halves(cast_w2, quant_w2, 1)
+        finish(1, 0)
+        store_y(1, 0)
+        requantize(0, 0)
+        both_halves(cast_x, quant_x, 3)
+        whole(1, 1, 0)
+        store_y(1, 1)
+        requantize(0, 1)
+        nc.sync.dma_start(out=out_words[:, 0, 0 : 2 * NT], in_=y_codes[0][:, 0, :])
+        whole(0, 2, 4)
+        store_y(0, 2)
+        requantize(1, 0)
+        requantize(1, 1)
+        nc.sync.dma_start(out=out_words[:, 1, 0 : 2 * NT], in_=y_codes[0][:, 1, :])
+        store_scales(0)
+        whole(1, 2, 0)
+        store_y(1, 2)
+        requantize(0, 2)
+        requantize(1, 2)
+        nc.sync.dma_start(out=out_words[:, :, 2 * NT : T], in_=y_codes[1][:])
+        store_scales(1)

@@ -28,7 +28,7 @@ def tile_mix_dconv_fm_pl_silu_kernel(
     w2_rows = w2.rearrange("(p j) n -> p j n", j=PACK)
     out_rows = out_0.rearrange("(a p r) t -> a p r t", a=GROUPS, r=PACK)
     out_words = out_1.rearrange("a p t i -> p a (t i)").bitcast(I32)
-    out_scales = out_2.rearrange("a q t -> q a t").bitcast(I32)
+    out_scales = out_2.bitcast(I32)
 
     with ExitStack() as ctx:
         sb = ctx.enter_context(tc.tile_pool(name="sb", bufs=1))
@@ -45,7 +45,8 @@ def tile_mix_dconv_fm_pl_silu_kernel(
         w0_raw = tile("w0_raw", [P, 2 * M], U8)
         w1_raw = tile("w1_raw", [P, M], I32)
         w2_raw = [tile("w2_raw%d" % a, [P, PACK, NT], F32) for a in range(GROUPS)]
-        x_raw = [tile("x_raw%d" % c, [P, PACK, NT], F32) for c in range(4)]
+        x_head = [tile("x_head%d" % h, [P, PACK, HALF], F32) for h in range(2)]
+        x_raw = {c: tile("x_raw%d" % c, [P, PACK, NT], F32) for c in range(1, 4)}
         w0_codes = tile("w0_codes", [P, 2 * M], U8)
         w1_codes = tile("w1_codes", [P, M], I32)
         w2_codes = tile("w2_codes", [P, M], I32)
@@ -53,19 +54,22 @@ def tile_mix_dconv_fm_pl_silu_kernel(
         x_codes = tile("x_codes", [P, T + 2 * D], I32)
         x_scale = tile("x_scale", [P, T + 2 * D], U8)
         y = {(a, tt): tile("y%d%d" % (a, tt), [P, PACK, NT], F32) for a in range(GROUPS) for tt in range(3)}
-        y_codes = [tile("y_codes0", [P, GROUPS, 2 * NT], I32), tile("y_codes1", [P, GROUPS, NT], I32)]
-        y_scale = [tile("y_scale0", [P, GROUPS, 2 * NT], U8), tile("y_scale1", [P, GROUPS, NT], U8)]
+        y_codes = [tile("y_codes%d" % a, [P, T], I32) for a in range(GROUPS)]
+        y_scale = tile("y_scale", [P, T], U8)
         staged = {}
         banks = {}
 
         def load_scales(tap, scales, quad):
             nc.sync.dma_start(
-                out=scale_raw[32 * quad : 32 * quad + 4, tap, :].bitcast(I32),
+                out=scale_raw[32 * quad + 4 * tap : 32 * quad + 4 * tap + 4, tap, :].bitcast(I32),
                 in_=scales[0, 4 * quad : 4 * quad + 4, :].bitcast(I32),
             )
 
         def load_x(c):
             nc.sync.dma_start(out=x_raw[c][:], in_=x_rows[:, :, NT * c : NT * (c + 1)])
+
+        def load_x_head(h):
+            nc.sync.dma_start(out=x_head[h][:], in_=x_rows[:, :, HALF * h : HALF * (h + 1)])
 
         def load_w2(a):
             nc.sync.dma_start(out=w2_raw[a][:], in_=w2_rows[:, :, NT * a : NT * (a + 1)])
@@ -76,12 +80,12 @@ def tile_mix_dconv_fm_pl_silu_kernel(
             else:
                 nc.vector.tensor_copy(out=out, in_=in_)
 
-        def interleave(engine, key, src, h):
-            grouped = tile("g_%s" % key, [P, HALF, PACK], BF16)
+        def interleave(engine, key, src):
+            grouped = tile("g_%s" % key, [P, src.shape[2], PACK], BF16)
             copy(
                 engine,
                 grouped[:].rearrange("p (c i) j -> p c j i", i=4),
-                src[:, :, HALF * h : HALF * (h + 1)].rearrange("p j (c i) -> p c j i", i=4),
+                src.rearrange("p j (c i) -> p c j i", i=4),
             )
             staged[key] = grouped[:].rearrange("p c j -> p (c j)")
 
@@ -89,7 +93,8 @@ def tile_mix_dconv_fm_pl_silu_kernel(
             nc.vector.quantize_mx(out=codes.bitcast(FP8X4), scales=scales, in_=staged[key])
 
         def cast_x(engine, c, h):
-            interleave(engine, "x%d%d" % (c, h), x_raw[c], h)
+            src = x_head[h][:] if c == 0 else x_raw[c][:, :, HALF * h : HALF * (h + 1)]
+            interleave(engine, "x%d%d" % (c, h), src)
 
         def quant_x(c, h):
             cols = slice(NT * c + HALF * h, NT * c + HALF * (h + 1))
@@ -141,7 +146,7 @@ def tile_mix_dconv_fm_pl_silu_kernel(
             nc.tensor.matmul_mx(
                 out=banks[a, tt, r][:],
                 lhsT=lhsT,
-                lhsT_scale=w_scale[tap][:, n0 : n0 + P],
+                lhsT_scale=w_scale[tap][4 * (tap % 2) : P, n0 : n0 + P],
                 rhs=x_codes[:, cols].bitcast(FP8X4),
                 rhs_scale=x_scale[:, cols],
                 start=(tap == 0),
@@ -167,12 +172,18 @@ def tile_mix_dconv_fm_pl_silu_kernel(
                     tap_pass(tap, a, tt, r)
                 silu_out(a, tt, r)
 
-        def requantize(a, tt):
-            for h in range(2):
-                interleave("vector", "y%d%d%d" % (a, tt, h), y[a, tt], h)
-            for h in range(2):
-                c0 = NT * (tt % 2) + HALF * h
-                quantize("y%d%d%d" % (a, tt, h), y_codes[tt // 2][:, a, c0 : c0 + HALF], y_scale[tt // 2][:, a, c0 : c0 + HALF])
+        def cast_y(engine, a, tt, c0, c1):
+            interleave(engine, "y%d%d_%d" % (a, tt, c0), y[a, tt][:, :, c0:c1])
+
+        def quant_y(a, tt, c0, c1):
+            cols = slice(NT * tt + c0, NT * tt + c1)
+            quantize("y%d%d_%d" % (a, tt, c0), y_codes[a][:, cols], y_scale[4 * a : P, cols])
+
+        def requantize(a, tt, first_engine):
+            cast_y(first_engine, a, tt, 0, HALF)
+            cast_y("vector", a, tt, HALF, NT)
+            for c0 in (HALF, 0) if first_engine == "scalar" else (0, HALF):
+                quant_y(a, tt, c0, c0 + HALF)
 
         def both_halves(cast, quant, c):
             cast("vector", c, 0)
@@ -183,21 +194,23 @@ def tile_mix_dconv_fm_pl_silu_kernel(
         def store_y(a, tt):
             nc.sync.dma_start(out=out_rows[a, :, :, NT * tt : NT * (tt + 1)], in_=y[a, tt][:])
 
-        def store_scales(part):
-            c0, c1 = (0, 2 * NT // 4) if part == 0 else (2 * NT // 4, T // 4)
-            for quad in range(4):
-                nc.sync.dma_start(
-                    out=out_scales[4 * quad : 4 * quad + 4, :, c0:c1],
-                    in_=y_scale[part][32 * quad : 32 * quad + 4, :, :].bitcast(I32),
-                )
+        def store_words(a, c0, c1):
+            nc.sync.dma_start(out=out_words[:, a, c0:c1], in_=y_codes[a][:, c0:c1])
+
+        def store_scales(engine, quad):
+            engine.dma_start(
+                out=out_scales[:, 4 * quad : 4 * quad + 4, :],
+                in_=y_scale[32 * quad : 32 * quad + 8, :].bitcast(I32),
+            )
 
         nc.vector.memset(scale_raw[:].rearrange("p s n -> p (s n)").bitcast(I32), 0)
         nc.vector.memset(warm_in[:], 0.0)
         nc.scalar.activation(out=warm_out[:], in_=warm_in[:], func=SILU)
-        nc.sync.dma_start(out=w0_raw[:].bitcast(I32), in_=w0_words[0].bitcast(I32))
+        load_x_head(0)
         for quad in range(4):
             load_scales(0, w0_scales, quad)
-        load_x(0)
+        nc.sync.dma_start(out=w0_raw[:].bitcast(I32), in_=w0_words[0].bitcast(I32))
+        load_x_head(1)
         nc.sync.dma_start(out=w1_raw[:], in_=w1_words[0].rearrange("p n i -> p (n i)").bitcast(I32))
         for quad in range(4):
             load_scales(1, w1_scales, quad)
@@ -208,16 +221,16 @@ def tile_mix_dconv_fm_pl_silu_kernel(
         load_w2(1)
         load_x(3)
 
+        cast_x("scalar", 0, 0)
         deal_scales(0)
         deal_w0(0)
-        cast_x("vector", 0, 0)
-        cast_x("scalar", 0, 1)
-        deal_w0(1)
+        cast_x("vector", 0, 1)
         quant_x(0, 0)
         quant_x(0, 1)
         open_banks(0, 0, 0)
         open_banks(1, 0, 4)
         tap_sweep(0, 0, 0)
+        deal_w0(1)
         tap_sweep(0, 1, 0)
         deal_w1()
         deal_scales(1)
@@ -242,21 +255,37 @@ def tile_mix_dconv_fm_pl_silu_kernel(
         both_halves(cast_w2, quant_w2, 1)
         finish(1, 0)
         store_y(1, 0)
-        requantize(0, 0)
+        requantize(0, 0, "vector")
         both_halves(cast_x, quant_x, 3)
         whole(1, 1, 0)
         store_y(1, 1)
-        requantize(0, 1)
-        nc.sync.dma_start(out=out_words[:, 0, 0 : 2 * NT], in_=y_codes[0][:, 0, :])
+        requantize(0, 1, "vector")
+        store_words(0, 0, 2 * NT)
+        requantize(1, 0, "vector")
+        requantize(1, 1, "scalar")
         whole(0, 2, 4)
         store_y(0, 2)
-        requantize(1, 0)
-        requantize(1, 1)
-        nc.sync.dma_start(out=out_words[:, 1, 0 : 2 * NT], in_=y_codes[0][:, 1, :])
-        store_scales(0)
-        whole(1, 2, 0)
-        store_y(1, 2)
-        requantize(0, 2)
-        requantize(1, 2)
-        nc.sync.dma_start(out=out_words[:, :, 2 * NT : T], in_=y_codes[1][:])
-        store_scales(1)
+        store_words(1, 0, 2 * NT)
+        requantize(0, 2, "vector")
+        store_words(0, 2 * NT, T)
+        open_banks(1, 2, 0)
+        for r in range(PACK):
+            for tap in range(3):
+                tap_pass(tap, 1, 2, r)
+            if r < PACK - 1:
+                silu_out(1, 2, r)
+        nc.sync.dma_start(out=out_rows[1, :, 0:3, 2 * NT : T], in_=y[1, 2][:, 0:3, :])
+        for c0 in (0, HALF):
+            nc.scalar.activation(
+                out=y[1, 2][:, 3, c0 : c0 + HALF], in_=banks[1, 2, 3][:, c0 : c0 + HALF], func=SILU, bias=bias[:, 1, 3:4]
+            )
+        nc.sync.dma_start(out=out_rows[1, :, 3, 2 * NT : T], in_=y[1, 2][:, 3, :])
+        cast_y("vector", 1, 2, 0, HALF)
+        cast_y("vector", 1, 2, HALF, 384)
+        cast_y("scalar", 1, 2, 384, NT)
+        quant_y(1, 2, 0, HALF)
+        quant_y(1, 2, HALF, 384)
+        quant_y(1, 2, 384, NT)
+        store_words(1, 2 * NT, T)
+        for quad in range(4):
+            store_scales(nc.scalar if quad < 2 else nc.sync, quad)

@@ -45,8 +45,8 @@ def tile_mix_dconv_fm_pl_silu_kernel(
         w0_raw = tile("w0_raw", [P, 2 * M], U8)
         w1_raw = tile("w1_raw", [P, M], I32)
         w2_raw = [tile("w2_raw%d" % a, [P, PACK, NT], F32) for a in range(GROUPS)]
-        x_head = [tile("x_head%d" % h, [P, PACK, HALF], F32) for h in range(2)]
-        x_raw = {c: tile("x_raw%d" % c, [P, PACK, NT], F32) for c in range(1, 4)}
+        x_half = {(c, h): tile("x_half%d%d" % (c, h), [P, PACK, HALF], F32) for c in (0, 2) for h in range(2)}
+        x_raw = {c: tile("x_raw%d" % c, [P, PACK, NT], F32) for c in (1, 3)}
         w0_codes = tile("w0_codes", [P, 2 * M], U8)
         w1_codes = tile("w1_codes", [P, M], I32)
         w2_codes = tile("w2_codes", [P, M], I32)
@@ -68,8 +68,9 @@ def tile_mix_dconv_fm_pl_silu_kernel(
         def load_x(c):
             nc.sync.dma_start(out=x_raw[c][:], in_=x_rows[:, :, NT * c : NT * (c + 1)])
 
-        def load_x_head(h):
-            nc.sync.dma_start(out=x_head[h][:], in_=x_rows[:, :, HALF * h : HALF * (h + 1)])
+        def load_x_half(c, h):
+            c0 = NT * c + HALF * h
+            nc.sync.dma_start(out=x_half[c, h][:], in_=x_rows[:, :, c0 : c0 + HALF])
 
         def load_w2(a):
             nc.sync.dma_start(out=w2_raw[a][:], in_=w2_rows[:, :, NT * a : NT * (a + 1)])
@@ -93,7 +94,7 @@ def tile_mix_dconv_fm_pl_silu_kernel(
             nc.vector.quantize_mx(out=codes.bitcast(FP8X4), scales=scales, in_=staged[key])
 
         def cast_x(engine, c, h):
-            src = x_head[h][:] if c == 0 else x_raw[c][:, :, HALF * h : HALF * (h + 1)]
+            src = x_half[c, h][:] if c % 2 == 0 else x_raw[c][:, :, HALF * h : HALF * (h + 1)]
             interleave(engine, "x%d%d" % (c, h), src)
 
         def quant_x(c, h):
@@ -191,8 +192,12 @@ def tile_mix_dconv_fm_pl_silu_kernel(
             quant(c, 0)
             quant(c, 1)
 
-        def store_y(a, tt):
-            nc.sync.dma_start(out=out_rows[a, :, :, NT * tt : NT * (tt + 1)], in_=y[a, tt][:])
+        def store_y(a, tt, r0, r1):
+            nc.sync.dma_start(out=out_rows[a, :, r0:r1, NT * tt : NT * (tt + 1)], in_=y[a, tt][:, r0:r1, :])
+
+        def store_halves(a, tt):
+            store_y(a, tt, 0, 2)
+            store_y(a, tt, 2, 4)
 
         def store_words(a, c0, c1):
             nc.sync.dma_start(out=out_words[:, a, c0:c1], in_=y_codes[a][:, c0:c1])
@@ -203,34 +208,36 @@ def tile_mix_dconv_fm_pl_silu_kernel(
                 in_=y_scale[32 * quad : 32 * quad + 8, :].bitcast(I32),
             )
 
-        nc.vector.memset(scale_raw[:].rearrange("p s n -> p (s n)").bitcast(I32), 0)
+        for tap in range(2):
+            nc.vector.memset(scale_raw[:, tap, :].bitcast(I32), 0)
         nc.vector.memset(warm_in[:], 0.0)
         nc.scalar.activation(out=warm_out[:], in_=warm_in[:], func=SILU)
-        load_x_head(0)
+        nc.sync.dma_start(out=w0_raw[:].bitcast(I32), in_=w0_words[0].bitcast(I32))
         for quad in range(4):
             load_scales(0, w0_scales, quad)
-        nc.sync.dma_start(out=w0_raw[:].bitcast(I32), in_=w0_words[0].bitcast(I32))
-        load_x_head(1)
+        load_x_half(0, 0)
+        load_x_half(0, 1)
         nc.sync.dma_start(out=w1_raw[:], in_=w1_words[0].rearrange("p n i -> p (n i)").bitcast(I32))
         for quad in range(4):
             load_scales(1, w1_scales, quad)
         load_x(1)
         nc.sync.dma_start(out=bias[:, :, 0:PACK], in_=b.rearrange("(a p r) -> p a r", a=GROUPS, r=PACK))
         load_w2(0)
-        load_x(2)
         load_w2(1)
+        load_x_half(2, 0)
+        load_x_half(2, 1)
         load_x(3)
 
-        cast_x("scalar", 0, 0)
-        deal_scales(0)
         deal_w0(0)
+        deal_scales(0)
+        deal_w0(1)
+        cast_x("scalar", 0, 0)
         cast_x("vector", 0, 1)
         quant_x(0, 0)
         quant_x(0, 1)
         open_banks(0, 0, 0)
         open_banks(1, 0, 4)
         tap_sweep(0, 0, 0)
-        deal_w0(1)
         tap_sweep(0, 1, 0)
         deal_w1()
         deal_scales(1)
@@ -245,30 +252,45 @@ def tile_mix_dconv_fm_pl_silu_kernel(
         quant_w2(0, 0)
         quant_w2(0, 1)
         finish(0, 0)
-        store_y(0, 0)
+        store_halves(0, 0)
         open_banks(0, 1, 0)
-        tap_sweep(0, 0, 1)
-        both_halves(cast_x, quant_x, 2)
+        cast_w2("vector", 1, 0)
+        cast_w2("vector", 1, 1)
+        quant_w2(1, 0)
+        cast_x("vector", 2, 0)
+        quant_w2(1, 1)
+        quant_x(2, 0)
+        for r0 in (0, 2):
+            for r in (r0, r0 + 1):
+                tap_pass(0, 0, 1, r)
+            for r in (r0, r0 + 1):
+                tap_pass(2, 1, 0, r)
+                silu_out(1, 0, r)
+        store_halves(1, 0)
         tap_sweep(1, 0, 1)
+        cast_x("vector", 2, 1)
+        cast_y("vector", 0, 0, 0, HALF)
+        quant_x(2, 1)
         finish(0, 1)
-        store_y(0, 1)
-        both_halves(cast_w2, quant_w2, 1)
-        finish(1, 0)
-        store_y(1, 0)
-        requantize(0, 0, "vector")
+        cast_y("vector", 0, 0, HALF, NT)
+        quant_y(0, 0, 0, HALF)
+        quant_y(0, 0, HALF, NT)
+        store_words(0, 0, NT)
+        store_halves(0, 1)
         both_halves(cast_x, quant_x, 3)
-        whole(1, 1, 0)
-        store_y(1, 1)
-        requantize(0, 1, "vector")
-        store_words(0, 0, 2 * NT)
+        whole(1, 1, 4)
         requantize(1, 0, "vector")
+        store_words(1, 0, NT)
+        store_halves(1, 1)
+        requantize(0, 1, "vector")
+        store_words(0, NT, 2 * NT)
         requantize(1, 1, "scalar")
-        whole(0, 2, 4)
-        store_y(0, 2)
-        store_words(1, 0, 2 * NT)
+        whole(0, 2, 0)
+        store_halves(0, 2)
+        store_words(1, NT, 2 * NT)
         requantize(0, 2, "vector")
         store_words(0, 2 * NT, T)
-        open_banks(1, 2, 0)
+        open_banks(1, 2, 4)
         for r in range(PACK):
             for tap in range(3):
                 tap_pass(tap, 1, 2, r)

from contextlib import ExitStack

import concourse.mybir as mybir

D, K, M, T = 256, 512, 1024, 1536
FLOPS = 2 * 3 * K * M * T

F32 = mybir.dt.float32
BF16 = mybir.dt.bfloat16
I32 = mybir.dt.int32
U8 = mybir.dt.uint8
FP8X4 = mybir.dt.float8_e4m3fn_x4
FP4X4 = mybir.dt.float4_e2m1fn_x4
SILU = mybir.ActivationFunctionType.Silu

P = 128
PACK = 4
NT = 512
HALF = 256
GROUPS = M // (P * PACK)


def tile_mix_dconv_fm_pl_silu_kernel(
    tc, x, w0_words, w0_scales, w1_words, w1_scales, w2, b, out_0, out_1, out_2
):
    nc = tc.nc
    x_rows = x.rearrange("(p j) t -> p j t", j=PACK)
    w2_rows = w2.rearrange("(p j) n -> p j n", j=PACK)
    out_rows = out_0.rearrange("(a p r) t -> a p r t", a=GROUPS, r=PACK)
    out_words = out_1.rearrange("a p t i -> p a (t i)").bitcast(I32)
    out_scales = out_2.bitcast(I32)

    with ExitStack() as ctx:
        sb = ctx.enter_context(tc.tile_pool(name="sb", bufs=1))
        psum = ctx.enter_context(tc.psum_pool(name="psum", bufs=1))
        ctx.enter_context(tc.manual_schedule())

        def tile(name, shape, dtype):
            return sb.tile(shape, dtype, name=name, align_bytes=64)

        warm_in = tile("warm_in", [P, 1], F32)
        warm_out = tile("warm_out", [P, 1], F32)
        bias = tile("bias", [P, GROUPS, 2 * PACK], F32)
        scale_raw = tile("scale_raw", [P, 2, M], U8)
        w0_raw = tile("w0_raw", [P, 2 * M], U8)
        w1_raw = tile("w1_raw", [P, M], I32)
        w2_raw = [tile("w2_raw%d" % a, [P, PACK, NT], F32) for a in range(GROUPS)]
        x_half = {(c, h): tile("x_half%d%d" % (c, h), [P, PACK, HALF], F32) for c in (0, 2) for h in range(2)}
        x_raw = {c: tile("x_raw%d" % c, [P, PACK, NT], F32) for c in (1, 3)}
        w0_codes = tile("w0_codes", [P, 2 * M], U8)
        w1_codes = tile("w1_codes", [P, M], I32)
        w2_codes = tile("w2_codes", [P, M], I32)
        w_scale = [tile("w_scale%d" % tap, [P, M], U8) for tap in range(3)]
        x_codes = tile("x_codes", [P, T + 2 * D], I32)
        x_scale = tile("x_scale", [P, T + 2 * D], U8)
        y = {(a, tt): tile("y%d%d" % (a, tt), [P, PACK, NT], F32) for a in range(GROUPS) for tt in range(3)}
        y_codes = [tile("y_codes%d" % a, [P, T], I32) for a in range(GROUPS)]
        y_scale = tile("y_scale", [P, T], U8)
        staged = {}
        banks = {}

        def load_scales(tap, scales, quad):
            nc.sync.dma_start(
                out=scale_raw[32 * quad + 4 * tap : 32 * quad + 4 * tap + 4, tap, :].bitcast(I32),
                in_=scales[0, 4 * quad : 4 * quad + 4, :].bitcast(I32),
            )

        def load_x(c):
            nc.sync.dma_start(out=x_raw[c][:], in_=x_rows[:, :, NT * c : NT * (c + 1)])

        def load_x_half(c, h):
            c0 = NT * c + HALF * h
            nc.sync.dma_start(out=x_half[c, h][:], in_=x_rows[:, :, c0 : c0 + HALF])

        def load_w2(a):
            nc.sync.dma_start(out=w2_raw[a][:], in_=w2_rows[:, :, NT * a : NT * (a + 1)])

        def copy(engine, out, in_):
            if engine == "scalar":
                nc.scalar.copy(out=out, in_=in_)
            else:
                nc.vector.tensor_copy(out=out, in_=in_)

        def interleave(engine, key, src):
            grouped = tile("g_%s" % key, [P, src.shape[2], PACK], BF16)
            copy(
                engine,
                grouped[:].rearrange("p (c i) j -> p c j i", i=4),
                src.rearrange("p j (c i) -> p c j i", i=4),
            )
            staged[key] = grouped[:].rearrange("p c j -> p (c j)")

        def quantize(key, codes, scales):
            nc.vector.quantize_mx(out=codes.bitcast(FP8X4), scales=scales, in_=staged[key])

        def cast_x(engine, c, h):
            src = x_half[c, h][:] if c % 2 == 0 else x_raw[c][:, :, HALF * h : HALF * (h + 1)]
            interleave(engine, "x%d%d" % (c, h), src)

        def quant_x(c, h):
            cols = slice(NT * c + HALF * h, NT * c + HALF * (h + 1))
            quantize("x%d%d" % (c, h), x_codes[:, cols], x_scale[:, cols])

        def cast_w2(engine, a, h):
            grouped = tile("g_w%d%d" % (a, h), [P, 2, P, PACK], BF16)
            copy(
                engine,
                grouped[:].rearrange("p r m j -> p m r j"),
                w2_raw[a][:].rearrange("p j (m r) -> p m r j", r=PACK)[:, :, 2 * h : 2 * h + 2, :],
            )
            staged["w%d%d" % (a, h)] = grouped[:].rearrange("p r m j -> p (r m j)")

        def quant_w2(a, h):
            cols = slice(NT * a + HALF * h, NT * a + HALF * (h + 1))
            quantize("w%d%d" % (a, h), w2_codes[:, cols], w_scale[2][:, cols])

        def deal_scales(tap):
            nc.vector.tensor_copy(
                out=w_scale[tap][:].rearrange("p (a r m) -> p a r m", a=GROUPS, r=PACK),
                in_=scale_raw[:, tap, :].rearrange("p (a m r) -> p a r m", a=GROUPS, r=PACK),
            )

        def deal_w0(a):
            cols = slice(2 * NT * a, 2 * NT * (a + 1))
            nc.vector.tensor_copy(
                out=w0_codes[:, cols].rearrange("p (r m e) -> p r m e", r=PACK, e=2),
                in_=w0_raw[:, cols].rearrange("p (m r e) -> p r m e", r=PACK, e=2),
            )

        def deal_w1():
            nc.vector.tensor_copy(
                out=w1_codes[:].rearrange("p (a r m) -> p a m r", a=GROUPS, r=PACK),
                in_=w1_raw[:].rearrange("p (a m r) -> p a m r", a=GROUPS, r=PACK),
            )

        def open_banks(a, tt, first):
            for r in range(PACK):
                banks[a, tt, r] = psum.tile([P, NT], F32, name="acc%d%d%d" % (a, tt, r), tag="bank%d" % (first + r))

        def tap_pass(tap, a, tt, r):
            n0 = NT * a + P * r
            if tap == 0:
                lhsT = w0_codes[:, 2 * n0 : 2 * (n0 + P)].bitcast(FP4X4)
            else:
                lhsT = (w1_codes if tap == 1 else w2_codes)[:, n0 : n0 + P].bitcast(FP8X4)
            cols = slice(NT * tt + D * tap, NT * (tt + 1) + D * tap)
            nc.tensor.matmul_mx(
                out=banks[a, tt, r][:],
                lhsT=lhsT,
                lhsT_scale=w_scale[tap][4 * (tap % 2) : P, n0 : n0 + P],
                rhs=x_codes[:, cols].bitcast(FP8X4),
                rhs_scale=x_scale[:, cols],
                start=(tap == 0),
                stop=(tap == 2),
            )

        def tap_sweep(tap, a, tt):
            for r in range(PACK):
                tap_pass(tap, a, tt, r)

        def silu_out(a, tt, r):
            nc.scalar.activation(out=y[a, tt][:, r, :], in_=banks[a, tt, r][:], func=SILU, bias=bias[:, a, r : r + 1])

        def finish(a, tt):
            for r in range(PACK):
                tap_pass(2, a, tt, r)
                silu_out(a, tt, r)

        def whole(a, tt, first):
            open_banks(a, tt, first)
            for r in range(PACK):
                for tap in range(3):
                    tap_pass(tap, a, tt, r)
                silu_out(a, tt, r)

        def cast_y(engine, a, tt, c0, c1):
            interleave(engine, "y%d%d_%d" % (a, tt, c0), y[a, tt][:, :, c0:c1])

        def quant_y(a, tt, c0, c1):
            cols = slice(NT * tt + c0, NT * tt + c1)
            quantize("y%d%d_%d" % (a, tt, c0), y_codes[a][:, cols], y_scale[4 * a : P, cols])

        def requantize(a, tt, first_engine):
            cast_y(first_engine, a, tt, 0, HALF)
            cast_y("vector", a, tt, HALF, NT)
            for c0 in (HALF, 0) if first_engine == "scalar" else (0, HALF):
                quant_y(a, tt, c0, c0 + HALF)

        def both_halves(cast, quant, c):
            cast("vector", c, 0)
            cast("vector", c, 1)
            quant(c, 0)
            quant(c, 1)

        def store_y(a, tt, r0, r1):
            nc.sync.dma_start(out=out_rows[a, :, r0:r1, NT * tt : NT * (tt + 1)], in_=y[a, tt][:, r0:r1, :])

        def store_halves(a, tt):
            store_y(a, tt, 0, 2)
            store_y(a, tt, 2, 4)

        def store_words(a, c0, c1):
            nc.sync.dma_start(out=out_words[:, a, c0:c1], in_=y_codes[a][:, c0:c1])

        def store_scales(engine, quad):
            engine.dma_start(
                out=out_scales[:, 4 * quad : 4 * quad + 4, :],
                in_=y_scale[32 * quad : 32 * quad + 8, :].bitcast(I32),
            )

        for tap in range(2):
            nc.vector.memset(scale_raw[:, tap, :].bitcast(I32), 0)
        nc.vector.memset(warm_in[:], 0.0)
        nc.scalar.activation(out=warm_out[:], in_=warm_in[:], func=SILU)
        nc.sync.dma_start(out=w0_raw[:].bitcast(I32), in_=w0_words[0].bitcast(I32))
        for quad in range(4):
            load_scales(0, w0_scales, quad)
        load_x_half(0, 0)
        load_x_half(0, 1)
        nc.sync.dma_start(out=w1_raw[:], in_=w1_words[0].rearrange("p n i -> p (n i)").bitcast(I32))
        for quad in range(4):
            load_scales(1, w1_scales, quad)
        load_x(1)
        nc.sync.dma_start(out=bias[:, :, 0:PACK], in_=b.rearrange("(a p r) -> p a r", a=GROUPS, r=PACK))
        load_w2(0)
        load_w2(1)
        load_x_half(2, 0)
        load_x_half(2, 1)
        load_x(3)

        deal_w0(0)
        deal_scales(0)
        deal_w0(1)
        cast_x("scalar", 0, 0)
        cast_x("vector", 0, 1)
        quant_x(0, 0)
        quant_x(0, 1)
        open_banks(0, 0, 0)
        open_banks(1, 0, 4)
        tap_sweep(0, 0, 0)
        tap_sweep(0, 1, 0)
        deal_w1()
        deal_scales(1)
        cast_x("vector", 1, 0)
        cast_x("scalar", 1, 1)
        quant_x(1, 0)
        tap_sweep(1, 0, 0)
        tap_sweep(1, 1, 0)
        quant_x(1, 1)
        cast_w2("vector", 0, 0)
        cast_w2("scalar", 0, 1)
        quant_w2(0, 0)
        quant_w2(0, 1)
        finish(0, 0)
        store_halves(0, 0)
        open_banks(0, 1, 0)
        cast_w2("vector", 1, 0)
        cast_w2("vector", 1, 1)
        quant_w2(1, 0)
        cast_x("vector", 2, 0)
        quant_w2(1, 1)
        quant_x(2, 0)
        for r0 in (0, 2):
            for r in (r0, r0 + 1):
                tap_pass(0, 0, 1, r)
            for r in (r0, r0 + 1):
                tap_pass(2, 1, 0, r)
                silu_out(1, 0, r)
        store_halves(1, 0)
        tap_sweep(1, 0, 1)
        cast_x("vector", 2, 1)
        cast_y("vector", 0, 0, 0, HALF)
        quant_x(2, 1)
        finish(0, 1)
        cast_y("vector", 0, 0, HALF, NT)
        quant_y(0, 0, 0, HALF)
        quant_y(0, 0, HALF, NT)
        store_words(0, 0, NT)
        store_halves(0, 1)
        both_halves(cast_x, quant_x, 3)
        whole(1, 1, 4)
        requantize(1, 0, "vector")
        store_words(1, 0, NT)
        store_halves(1, 1)
        requantize(0, 1, "vector")
        store_words(0, NT, 2 * NT)
        requantize(1, 1, "scalar")
        whole(0, 2, 0)
        store_halves(0, 2)
        store_words(1, NT, 2 * NT)
        requantize(0, 2, "vector")
        store_words(0, 2 * NT, T)
        open_banks(1, 2, 4)
        for r in range(PACK):
            for tap in range(3):
                tap_pass(tap, 1, 2, r)
            if r < PACK - 1:
                silu_out(1, 2, r)
        nc.sync.dma_start(out=out_rows[1, :, 0:3, 2 * NT : T], in_=y[1, 2][:, 0:3, :])
        for c0 in (0, HALF):
            nc.scalar.activation(
                out=y[1, 2][:, 3, c0 : c0 + HALF], in_=banks[1, 2, 3][:, c0 : c0 + HALF], func=SILU, bias=bias[:, 1, 3:4]
            )
        nc.sync.dma_start(out=out_rows[1, :, 3, 2 * NT : T], in_=y[1, 2][:, 3, :])
        cast_y("vector", 1, 2, 0, HALF)
        cast_y("vector", 1, 2, HALF, 384)
        cast_y("scalar", 1, 2, 384, NT)
        quant_y(1, 2, 0, HALF)
        quant_y(1, 2, HALF, 384)
        quant_y(1, 2, 384, NT)
        store_words(1, 2 * NT, T)
        for quad in range(4):
            store_scales(nc.scalar if quad < 2 else nc.sync, quad)
